import numpy as np
import ml_dtypes


def mxq(x, axis, fmt="e4m3"):
    dtype, down = {"e4m3": (ml_dtypes.float8_e4m3fn, 7), "e5m2": (ml_dtypes.float8_e5m2, 14)}[fmt]
    v = np.moveaxis(np.asarray(x, np.float32).astype(ml_dtypes.bfloat16).astype(np.float64), axis, -1)
    blocks = v.reshape(v.shape[:-1] + (-1, 32))
    amax = np.abs(blocks).max(-1, keepdims=True)
    byte = np.maximum(np.where(amax > 0, np.frexp(amax)[1] - 1 + 127, 0) - down, 1)
    scale = np.exp2(byte - 127.0)
    codes = (blocks / scale).astype(np.float32).astype(dtype).astype(np.float64)
    return np.moveaxis((codes * scale).reshape(v.shape), -1, axis)


WIDE = False


def mx_kscale(k):
    if not WIDE:
        return np.ones(k)
    levels = np.array([10, -10, 5, -5, 0])
    if k % 512:
        return np.exp2(np.random.permutation(np.resize(levels, k // 32))).repeat(32)
    a = np.empty((k // 512, 16))
    for p in range(k // 512):
        a[p, :8] = np.random.permutation(np.resize(levels, 8))
        for g in range(8):
            far = levels[np.abs(levels - a[p, g]) >= 10]
            a[p, g + 8] = far[np.random.randint(len(far))]
    return np.exp2(a.ravel()).repeat(32)


def f64(x):
    return np.asarray(x).astype(np.float64)


def striped(idx):
    return np.tile(np.asarray(idx).reshape(-1, 16).T, (8, 1)).astype(np.uint16)


def unstriped(offs):
    return offs[:16].T.reshape(-1).astype(np.int64)


E2M1 = np.array([0.0, 0.5, 1.0, 1.5, 2.0, 3.0, 4.0, 6.0, -0.0, -0.5, -1.0, -1.5, -2.0, -3.0, -4.0, -6.0])


def pack_weight(w, fmt):
    k, n = w.shape
    w = f64(np.asarray(w, np.float32).astype(ml_dtypes.bfloat16)).reshape(k // 32, 32, n)
    amax = np.abs(w).max(1)
    if fmt == "e4m3":
        byte = np.frexp(amax)[1] - 1 + 127 - 7
    else:
        mant, ex = np.frexp(amax / 6.0)
        byte = np.where(mant > 0.5, ex, ex - 1) + 127
    byte = np.clip(np.where(amax > 0, byte, 1), 1, 254)
    scaled = (w * np.exp2(127.0 - byte)[:, None, :]).reshape(k, n).astype(np.float32)
    by_word = np.ascontiguousarray(scaled.reshape(k // 512, 128, 4, n).transpose(0, 1, 3, 2))
    if fmt == "e4m3":
        words = by_word.astype(ml_dtypes.float8_e4m3fn).view(np.uint8)
    else:
        c = by_word.astype(ml_dtypes.float4_e2m1fn).view(np.uint8) & 0xF
        words = (c[..., 0::2] | (c[..., 1::2] << 4)).reshape(k // 512, 128, 2 * n)
    return np.ascontiguousarray(words), np.ascontiguousarray(byte.astype(np.uint8).reshape(k // 512, 16, n))


def unpack_weight(words, scales, fmt):
    g, _, n = scales.shape
    words = np.ascontiguousarray(words).reshape(g, 128, n, -1)
    if fmt == "e4m3":
        vals = words.view(ml_dtypes.float8_e4m3fn).astype(np.float64)
    else:
        nib = np.empty((g, 128, n, 4), np.uint8)
        nib[..., 0::2] = words & 0xF
        nib[..., 1::2] = words >> 4
        vals = E2M1[nib]
    vals = vals * np.repeat(np.exp2(scales.astype(np.float64) - 127.0), 8, axis=1)[..., None]
    return vals.transpose(0, 1, 3, 2).reshape(g * 512, n)


def bf(x):
    return np.asarray(x, np.float32).astype(ml_dtypes.bfloat16)


def planes(Y):
    r, m = Y.shape
    b = f64(bf(Y)).reshape(r // 32, 32, m)
    amax = np.abs(b).max(1)
    byte = np.clip(np.where(amax > 0, np.frexp(amax)[1] - 1 + 127 - 7, 1), 1, 254)
    codes = (b * np.exp2(127.0 - byte)[:, None, :]).reshape(r, m).astype(np.float32).astype(ml_dtypes.float8_e4m3fn).view(np.uint8)
    words = codes.reshape(r // 512, 128, 4, m).transpose(0, 1, 3, 2)
    return np.ascontiguousarray(words), np.ascontiguousarray(byte.astype(np.uint8).reshape(r // 512, 16, m))


D, T, I, Q, E, X = 512, 2048, 512, 256, 512, 1024


def setup_inputs():
    n = np.random.standard_normal
    idx = np.random.permutation(T)[:I]
    idx2 = np.random.permutation(T)[:I]
    idx3 = np.random.permutation(X)[:I]
    fd = mx_kscale(D)
    fi = mx_kscale(I)
    keysp = pack_weight(n((D, T)) / fd[:, None], "e2m1")
    return {
        "query": (n((D, Q)) * 1.0 / np.sqrt(D) * fd[:, None]).astype(np.float32),
        "keys_words": keysp[0],
        "keys_scales": keysp[1],
        "os": (np.random.uniform(0.02, 0.08, (1, I)) * fi).astype(np.float32),
        "vals": (n((E, T))).astype(np.float32),
        "vals2": (n((E, X))).astype(np.float32),
        "vsc": (np.random.uniform(0.5, 2.0, (1, I)) / fi).astype(np.float32),
        "offs": striped(idx),
        "offs2": striped(idx2),
        "offs3": striped(idx3),
    }


def reference(query, keys_words, keys_scales, os, vals, vals2, vsc, offs, offs2, offs3):
    idx = unstriped(offs)
    idx2 = unstriped(offs2)
    idx3 = unstriped(offs3)
    keysu = unpack_weight(keys_words, keys_scales, "e2m1")
    queryq = mxq(f64(query), 0, "e4m3")
    a = queryq.T @ keysu
    w = a[:, idx] - a[:, idx2]
    wo1 = w * f64(os)
    wt1 = wo1.T
    vz = np.abs(f64(vals)[:, idx] - f64(vals2)[:, idx3]) * f64(vsc)
    vt1 = vz.T
    vt1q = mxq(vt1, 0, "e4m3")
    wt1q = mxq(wt1, 0, "e4m3")
    o = vt1q.T @ wt1q
    words, scales = planes(o)
    return o, words, scales

@@ -1,0 +1,222 @@
+from contextlib import ExitStack
+
+import concourse.mybir as mybir
+from concourse.masks import make_identity
+
+D, T, I, Q, E, X = 512, 2048, 512, 256, 512, 1024
+FLOPS = 2 * D * Q * T + 2 * I * E * Q
+
+F32 = mybir.dt.float32
+BF16 = mybir.dt.bfloat16
+I32 = mybir.dt.int32
+U32 = mybir.dt.uint32
+U16 = mybir.dt.uint16
+U8 = mybir.dt.uint8
+FP8X4 = mybir.dt.float8_e4m3fn_x4
+FP4X4 = mybir.dt.float4_e2m1fn_x4
+ALU = mybir.AluOpType
+ACT = mybir.ActivationFunctionType
+
+P = 128
+PACK = 4
+BANK = 512
+
+
+def tile_attend_difference_apartvalues_lean_pl_kernel(
+    tc, query, keys_words, keys_scales, wfac, vals, vals2, vfac, offs, offs2, offs3, out_0, out_1, out_2
+):
+    nc = tc.nc
+    with ExitStack() as ctx:
+        keep = ctx.enter_context(tc.tile_pool(name="keep", bufs=1))
+        work = ctx.enter_context(tc.tile_pool(name="work", bufs=2))
+        ps_a = ctx.enter_context(tc.psum_pool(name="ps_a", bufs=4))
+        ps_t = ctx.enter_context(tc.psum_pool(name="ps_t", bufs=2))
+        ps_o = ctx.enter_context(tc.psum_pool(name="ps_o", bufs=2))
+
+        list1 = keep.tile([P, I // 16], U16, name="list1")
+        list2 = keep.tile([P, I // 16], U16, name="list2")
+        list3 = keep.tile([P, I // 16], U16, name="list3")
+        q_raw = keep.tile([P, PACK, Q], F32, name="q_raw")
+        k_words = keep.tile([P, 2 * T], U8, name="k_words", align_bytes=64)
+        k_scales = keep.tile([P, T], U8, name="k_scales", align_bytes=64)
+        wfac_sb = keep.tile([P, PACK], F32, name="wfac_sb")
+        vfac_sb = keep.tile([P, PACK], F32, name="vfac_sb")
+        va = [keep.tile([P, T], F32, name="va%d" % j) for j in range(PACK)]
+        vb = [keep.tile([P, X], F32, name="vb%d" % j) for j in range(PACK)]
+        vals_j = vals.rearrange("(p j) t -> p j t", j=PACK)
+        vals2_j = vals2.rearrange("(p j) t -> p j t", j=PACK)
+
+        nc.sync.dma_start(out=q_raw[:], in_=query.rearrange("(p j) q -> p j q", j=PACK))
+        for g in range(4):
+            nc.sync.dma_start(
+                out=k_scales[32 * g : 32 * g + 4, :].bitcast(I32),
+                in_=keys_scales[0, 4 * g : 4 * g + 4, :].bitcast(I32),
+            )
+        nc.sync.dma_start(out=k_words[:].bitcast(I32), in_=keys_words[0].bitcast(I32))
+        nc.sync.dma_start(list3[:], offs3)
+        nc.sync.dma_start(out=vb[0][:], in_=vals2_j[:, 0, :])
+        nc.sync.dma_start(list2[:], offs2)
+        nc.sync.dma_start(list1[:], offs)
+        nc.sync.dma_start(out=va[0][:], in_=vals_j[:, 0, :])
+        nc.gpsimd.dma_start(out=wfac_sb[:], in_=wfac.rearrange("o (p t) -> (o p) t", t=PACK))
+        nc.gpsimd.dma_start(out=vfac_sb[:], in_=vfac.rearrange("o (p t) -> (o p) t", t=PACK))
+        for j in range(1, PACK):
+            nc.sync.dma_start(out=vb[j][:], in_=vals2_j[:, j, :])
+            nc.sync.dma_start(out=va[j][:], in_=vals_j[:, j, :])
+
+        ident = keep.tile([P, P], F32, name="ident")
+        make_identity(nc, ident[:])
+
+        q_bf = keep.tile([P, Q, PACK], BF16, name="q_bf", align_bytes=64)
+        nc.vector.tensor_copy(
+            out=q_bf[:].rearrange("p (c i) t -> p c t i", i=4),
+            in_=q_raw[:].rearrange("p t (c i) -> p c t i", i=4),
+        )
+        q_codes = keep.tile([P, Q], U32, name="q_codes", align_bytes=64)
+        q_scales = keep.tile([P, Q], U8, name="q_scales", align_bytes=64)
+        nc.vector.quantize_mx(
+            out=q_codes[:].bitcast(FP8X4), scales=q_scales[:], in_=q_bf[:].rearrange("p q t -> p (q t)")
+        )
+
+        scores = [keep.tile([P, T], F32, name="scores%d" % h) for h in range(Q // P)]
+
+        def score(h, on_vector):
+            rows = slice(h * P, (h + 1) * P)
+            for c in range(T // BANK):
+                acc = ps_a.tile([P, BANK], F32, name="acc")
+                nc.tensor.matmul_mx(
+                    out=acc[:],
+                    lhsT=q_codes[:, rows].bitcast(FP8X4),
+                    lhsT_scale=q_scales[:, rows],
+                    rhs=k_words[:, 2 * BANK * c : 2 * BANK * (c + 1)].bitcast(FP4X4),
+                    rhs_scale=k_scales[:, BANK * c : BANK * (c + 1)],
+                    start=True,
+                    stop=True,
+                )
+                if c in on_vector:
+                    nc.vector.tensor_copy(out=scores[h][:, BANK * c : BANK * (c + 1)], in_=acc[:])
+                else:
+                    nc.scalar.copy(out=scores[h][:, BANK * c : BANK * (c + 1)], in_=acc[:])
+
+        def pick(window, offsets, got, on_vector=False):
+            if on_vector:
+                nc.vector.tensor_copy(out=got, in_=window[:].indirect(offsets[:]))
+            else:
+                nc.scalar.activation(out=got, in_=window[:].indirect(offsets[:]), func=ACT.Copy)
+
+        def difference(window, other, diff):
+            nc.vector.tensor_tensor(out=diff, in0=window[:].indirect(list1[:]), in1=other, op=ALU.subtract)
+
+        def turn(places):
+            turned = ps_t.tile([P, PACK, P], F32, name="turned")
+            for t in range(PACK):
+                nc.tensor.transpose(turned[:, t, :], places[t], ident[:])
+            return turned
+
+        def turn_weights(diff):
+            return turn([diff[:, t::PACK] for t in range(PACK)])
+
+        def turn_values(diff):
+            size = work.tile([P, PACK, P], F32, name="size")
+            nc.scalar.activation(
+                out=size[:].rearrange("p t s -> p s t"),
+                in_=diff.rearrange("p (s t) -> p s t", t=PACK),
+                func=ACT.Abs,
+            )
+            return turn([size[:, t, :] for t in range(PACK)])
+
+        def scale_round(turned, factor, dst):
+            nc.vector.tensor_tensor(
+                out=dst.rearrange("p (c t) -> p c t", t=PACK),
+                in0=turned[:].rearrange("p t c -> p c t"),
+                in1=factor[:].unsqueeze(1).to_broadcast([P, P, PACK]),
+                op=ALU.mult,
+            )
+
+        def quantise(src, name):
+            width = src.shape[1] // PACK
+            codes = keep.tile([P, width], U32, name=name + "_codes", align_bytes=64)
+            scales = keep.tile([P, width], U8, name=name + "_scales", align_bytes=64)
+            nc.vector.quantize_mx(out=codes[:].bitcast(FP8X4), scales=scales[:], in_=src)
+            return codes, scales
+
+        o_sb = keep.tile([P, PACK, Q], F32, name="o_sb")
+        out_j = out_0.rearrange("(p j) q -> p j q", j=PACK)
+
+        def product(j, v_mx, first, w_mx):
+            res = ps_o.tile([P, Q], F32, name="res")
+            nc.tensor.matmul_mx(
+                out=res[:],
+                lhsT=v_mx[0][:, first : first + P].bitcast(FP8X4),
+                lhsT_scale=v_mx[1][:, first : first + P],
+                rhs=w_mx[0][:].bitcast(FP8X4),
+                rhs_scale=w_mx[1][:],
+                start=True,
+                stop=True,
+            )
+            nc.scalar.copy(out=o_sb[:, j, :], in_=res[:])
+
+        unit = I // 2
+        room_x = keep.tile([P, 6 * unit], F32, name="room_x", align_bytes=64)
+        room_y = keep.tile([P, 6 * unit], F32, name="room_y", align_bytes=64)
+
+        def wide(room, first):
+            return room[:, first * unit : (first + 2) * unit]
+
+        def rounded(room, first, count=1):
+            return room[:, first * unit : (first + count) * unit].bitcast(BF16)
+
+        pick(vb[0], list3, wide(room_x, 4))
+        score(0, (0, 1, 2))
+        pick(scores[0], list2, wide(room_x, 1))
+        score(1, (0, 2))
+        difference(va[0], wide(room_x, 4), wide(room_y, 3))
+        t_v0 = turn_values(wide(room_y, 3))
+        pick(scores[1], list2, wide(room_y, 1))
+        difference(scores[0], wide(room_x, 1), wide(room_x, 3))
+        scale_round(t_v0, vfac_sb, rounded(room_x, 2))
+        t_w0 = turn_weights(wide(room_x, 3))
+        pick(vb[1], list3, wide(room_y, 3))
+        difference(scores[1], wide(room_y, 1), wide(room_x, 0))
+        scale_round(t_w0, wfac_sb, rounded(room_y, 2))
+        t_w1 = turn_weights(wide(room_x, 0))
+        pick(vb[2], list3, wide(room_x, 3))
+        difference(va[1], wide(room_y, 3), wide(room_y, 0))
+        scale_round(t_w1, wfac_sb, rounded(room_y, 3))
+        t_v1 = turn_values(wide(room_y, 0))
+        w_mx = quantise(rounded(room_y, 2, 2), "w")
+        pick(vb[3], list3, wide(room_y, 0))
+        difference(va[2], wide(room_x, 3), wide(room_y, 4))
+        scale_round(t_v1, vfac_sb, rounded(room_x, 3))
+        t_v2 = turn_values(wide(room_y, 4))
+        v01_mx = quantise(rounded(room_x, 2, 2), "v01")
+        product(0, v01_mx, 0, w_mx)
+        product(1, v01_mx, P, w_mx)
+        difference(va[3], wide(room_y, 0), wide(room_x, 4))
+        scale_round(t_v2, vfac_sb, rounded(room_y, 0))
+        t_v3 = turn_values(wide(room_x, 4))
+        product(2, quantise(rounded(room_y, 0), "v2"), 0, w_mx)
+        nc.sync.dma_start(out=out_j[:, : PACK - 1, :], in_=o_sb[:, : PACK - 1, :])
+        scale_round(t_v3, vfac_sb, rounded(room_y, 1))
+        product(3, quantise(rounded(room_y, 1), "v3"), 0, w_mx)
+        nc.sync.dma_start(out=out_j[:, PACK - 1, :], in_=o_sb[:, PACK - 1, :])
+
+        o_bf = keep.tile([P, Q, PACK], BF16, name="o_bf", align_bytes=64)
+        nc.vector.tensor_copy(
+            out=o_bf[:].rearrange("p (c i) t -> p c t i", i=4),
+            in_=o_sb[:].rearrange("p t (c i) -> p c t i", i=4),
+        )
+        o_codes = keep.tile([P, Q], U32, name="o_codes", align_bytes=64)
+        o_scales = keep.tile([P, Q], U8, name="o_scales", align_bytes=64)
+        nc.vector.quantize_mx(
+            out=o_codes[:].bitcast(FP8X4), scales=o_scales[:], in_=o_bf[:].rearrange("p q t -> p (q t)")
+        )
+        nc.sync.dma_start(
+            out=out_1[0].rearrange("p q t -> p (q t)").bitcast(I32), in_=o_codes[:].bitcast(I32)
+        )
+        for g in range(4):
+            queue = nc.scalar if g % 2 == 0 else nc.sync
+            queue.dma_start(
+                out=out_2[0, 4 * g : 4 * g + 4, :].bitcast(I32),
+                in_=o_scales[32 * g : 32 * g + 4, :].bitcast(I32),
+            )

@@ -28,10 +28,9 @@ def tile_attend_difference_apartvalues_lean_pl_kernel(
     nc = tc.nc
     with ExitStack() as ctx:
         keep = ctx.enter_context(tc.tile_pool(name="keep", bufs=1))
-        work = ctx.enter_context(tc.tile_pool(name="work", bufs=2))
-        ps_a = ctx.enter_context(tc.psum_pool(name="ps_a", bufs=4))
-        ps_t = ctx.enter_context(tc.psum_pool(name="ps_t", bufs=2))
-        ps_o = ctx.enter_context(tc.psum_pool(name="ps_o", bufs=2))
+        ps_a = ctx.enter_context(tc.psum_pool(name="ps_a", bufs=3))
+        ps_t = ctx.enter_context(tc.psum_pool(name="ps_t", bufs=3))
+        ps_o = ctx.enter_context(tc.psum_pool(name="ps_o", bufs=1))
 
         list1 = keep.tile([P, I // 16], U16, name="list1")
         list2 = keep.tile([P, I // 16], U16, name="list2")
@@ -41,8 +40,8 @@ def tile_attend_difference_apartvalues_lean_pl_kernel(
         k_scales = keep.tile([P, T], U8, name="k_scales", align_bytes=64)
         wfac_sb = keep.tile([P, PACK], F32, name="wfac_sb")
         vfac_sb = keep.tile([P, PACK], F32, name="vfac_sb")
-        va = [keep.tile([P, T], F32, name="va%d" % j) for j in range(PACK)]
-        vb = [keep.tile([P, X], F32, name="vb%d" % j) for j in range(PACK)]
+        va = [keep.tile([P, T], F32, name="va%d" % j, tag="va%d" % j, align_bytes=64) for j in range(PACK)]
+        vb = [keep.tile([P, X], F32, name="vb%d" % j, tag="vb%d" % j, align_bytes=64) for j in range(PACK)]
         vals_j = vals.rearrange("(p j) t -> p j t", j=PACK)
         vals2_j = vals2.rearrange("(p j) t -> p j t", j=PACK)
 
@@ -52,9 +51,10 @@ def tile_attend_difference_apartvalues_lean_pl_kernel(
                 out=k_scales[32 * g : 32 * g + 4, :].bitcast(I32),
                 in_=keys_scales[0, 4 * g : 4 * g + 4, :].bitcast(I32),
             )
-        nc.sync.dma_start(out=k_words[:].bitcast(I32), in_=keys_words[0].bitcast(I32))
+        nc.sync.dma_start(out=k_words[:, :T].bitcast(I32), in_=keys_words[0, :, :T].bitcast(I32))
         nc.sync.dma_start(list3[:], offs3)
         nc.sync.dma_start(out=vb[0][:], in_=vals2_j[:, 0, :])
+        nc.sync.dma_start(out=k_words[:, T:].bitcast(I32), in_=keys_words[0, :, T:].bitcast(I32))
         nc.sync.dma_start(list2[:], offs2)
         nc.sync.dma_start(list1[:], offs)
         nc.sync.dma_start(out=va[0][:], in_=vals_j[:, 0, :])
@@ -67,45 +67,61 @@ def tile_attend_difference_apartvalues_lean_pl_kernel(
         ident = keep.tile([P, P], F32, name="ident")
         make_identity(nc, ident[:])
 
-        q_bf = keep.tile([P, Q, PACK], BF16, name="q_bf", align_bytes=64)
-        nc.vector.tensor_copy(
-            out=q_bf[:].rearrange("p (c i) t -> p c t i", i=4),
-            in_=q_raw[:].rearrange("p t (c i) -> p c t i", i=4),
-        )
+        q_bf = keep.tile([P, Q * PACK], BF16, name="q_bf", align_bytes=64)
         q_codes = keep.tile([P, Q], U32, name="q_codes", align_bytes=64)
         q_scales = keep.tile([P, Q], U8, name="q_scales", align_bytes=64)
-        nc.vector.quantize_mx(
-            out=q_codes[:].bitcast(FP8X4), scales=q_scales[:], in_=q_bf[:].rearrange("p q t -> p (q t)")
-        )
+        for h, rounding in enumerate((nc.vector.tensor_copy, nc.scalar.copy)):
+            rounding(
+                out=q_bf[:, h * BANK : (h + 1) * BANK].rearrange("p (c i t) -> p c t i", i=4, t=PACK),
+                in_=q_raw[:, :, h * P : (h + 1) * P].rearrange("p t (c i) -> p c t i", i=4),
+            )
+        for h in range(Q // P):
+            nc.vector.quantize_mx(
+                out=q_codes[:, h * P : (h + 1) * P].bitcast(FP8X4),
+                scales=q_scales[:, h * P : (h + 1) * P],
+                in_=q_bf[:, h * BANK : (h + 1) * BANK],
+            )
 
-        scores = [keep.tile([P, T], F32, name="scores%d" % h) for h in range(Q // P)]
+        scores = [keep.tile([P, T], F32, name="scores0")]
 
-        def score(h, on_vector):
+        def score(h, c, emptying):
             rows = slice(h * P, (h + 1) * P)
-            for c in range(T // BANK):
-                acc = ps_a.tile([P, BANK], F32, name="acc")
-                nc.tensor.matmul_mx(
-                    out=acc[:],
-                    lhsT=q_codes[:, rows].bitcast(FP8X4),
-                    lhsT_scale=q_scales[:, rows],
-                    rhs=k_words[:, 2 * BANK * c : 2 * BANK * (c + 1)].bitcast(FP4X4),
-                    rhs_scale=k_scales[:, BANK * c : BANK * (c + 1)],
-                    start=True,
-                    stop=True,
+            acc = ps_a.tile([P, BANK], F32, name="acc", tag="acc")
+            nc.tensor.matmul_mx(
+                out=acc[:],
+                lhsT=q_codes[:, rows].bitcast(FP8X4),
+                lhsT_scale=q_scales[:, rows],
+                rhs=k_words[:, 2 * BANK * c : 2 * BANK * (c + 1)].bitcast(FP4X4),
+                rhs_scale=k_scales[:, BANK * c : BANK * (c + 1)],
+                start=True,
+                stop=True,
+            )
+            emptying(out=scores[h][:, BANK * c : BANK * (c + 1)], in_=acc[:])
+
+        def pick(window, offsets, got, sign=1.0):
+            nc.scalar.activation(out=got, in_=window[:].indirect(offsets[:]), func=ACT.Copy, scale=sign)
+
+        def difference(window, other, diff, parts=1):
+            width = I // parts
+            for n in range(parts):
+                cols = slice(n * width, (n + 1) * width)
+                nc.vector.tensor_tensor(
+                    out=diff[:, cols],
+                    in0=window[:].indirect(list1[:, n * width // 16 : (n + 1) * width // 16]),
+                    in1=other[:, cols],
+                    op=ALU.subtract,
                 )
-                if c in on_vector:
-                    nc.vector.tensor_copy(out=scores[h][:, BANK * c : BANK * (c + 1)], in_=acc[:])
-                else:
-                    nc.scalar.copy(out=scores[h][:, BANK * c : BANK * (c + 1)], in_=acc[:])
 
-        def pick(window, offsets, got, on_vector=False):
-            if on_vector:
-                nc.vector.tensor_copy(out=got, in_=window[:].indirect(offsets[:]))
-            else:
-                nc.scalar.activation(out=got, in_=window[:].indirect(offsets[:]), func=ACT.Copy)
-
-        def difference(window, other, diff):
-            nc.vector.tensor_tensor(out=diff, in0=window[:].indirect(list1[:]), in1=other, op=ALU.subtract)
+        def turn_and_add(bank, term, first):
+            for t in range(PACK):
+                nc.tensor.matmul(
+                    bank[:, t, :],
+                    term[:, t::PACK],
+                    ident[:],
+                    start=first and t == 0,
+                    stop=not first and t == PACK - 1,
+                    is_transpose=True,
+                )
 
         def turn(places):
             turned = ps_t.tile([P, PACK, P], F32, name="turned")
@@ -116,13 +132,16 @@ def tile_attend_difference_apartvalues_lean_pl_kernel(
         def turn_weights(diff):
             return turn([diff[:, t::PACK] for t in range(PACK)])
 
-        def turn_values(diff):
-            size = work.tile([P, PACK, P], F32, name="size")
-            nc.scalar.activation(
-                out=size[:].rearrange("p t s -> p s t"),
-                in_=diff.rearrange("p (s t) -> p s t", t=PACK),
-                func=ACT.Abs,
-            )
+        def turn_values(diff, tag, parts=1):
+            size = keep.tile([P, PACK, P], F32, name="size", tag=tag, align_bytes=64)
+            width = P // parts
+            for n in range(parts):
+                rows = slice(n * width, (n + 1) * width)
+                nc.scalar.activation(
+                    out=size[:].rearrange("p t s -> p s t")[:, rows, :],
+                    in_=diff.rearrange("p (s t) -> p s t", t=PACK)[:, rows, :],
+                    func=ACT.Abs,
+                )
             return turn([size[:, t, :] for t in range(PACK)])
 
         def scale_round(turned, factor, dst):
@@ -140,25 +159,36 @@ def tile_attend_difference_apartvalues_lean_pl_kernel(
             nc.vector.quantize_mx(out=codes[:].bitcast(FP8X4), scales=scales[:], in_=src)
             return codes, scales
 
-        o_sb = keep.tile([P, PACK, Q], F32, name="o_sb")
         out_j = out_0.rearrange("(p j) q -> p j q", j=PACK)
 
+        res = [ps_o.tile([P, PACK, P], F32, name="res%d" % h) for h in range(Q // P)]
+
         def product(j, v_mx, first, w_mx):
-            res = ps_o.tile([P, Q], F32, name="res")
-            nc.tensor.matmul_mx(
-                out=res[:],
-                lhsT=v_mx[0][:, first : first + P].bitcast(FP8X4),
-                lhsT_scale=v_mx[1][:, first : first + P],
-                rhs=w_mx[0][:].bitcast(FP8X4),
-                rhs_scale=w_mx[1][:],
-                start=True,
-                stop=True,
-            )
-            nc.scalar.copy(out=o_sb[:, j, :], in_=res[:])
+            for h in range(Q // P):
+                nc.tensor.matmul_mx(
+                    out=res[h][:, j, :],
+                    lhsT=v_mx[0][:, first : first + P].bitcast(FP8X4),
+                    lhsT_scale=v_mx[1][:, first : first + P],
+                    rhs=w_mx[0][:, h * P : (h + 1) * P].bitcast(FP8X4),
+                    rhs_scale=w_mx[1][:, h * P : (h + 1) * P],
+                    start=True,
+                    stop=True,
+                )
+
+        def hand_out(tiles, banks):
+            for h in banks:
+                nc.scalar.copy(out=o_sb[:, tiles, h * P : (h + 1) * P], in_=res[h][:, tiles, :])
+            nc.sync.dma_start(out=out_j[:, tiles, :], in_=o_sb[:, tiles, :])
 
         unit = I // 2
-        room_x = keep.tile([P, 6 * unit], F32, name="room_x", align_bytes=64)
-        room_y = keep.tile([P, 6 * unit], F32, name="room_y", align_bytes=64)
+        room_a = keep.tile([P, 3 * unit], F32, name="room_a")
+        room_b = keep.tile([P, 3 * unit], F32, name="room_b")
+        room_c = keep.tile([P, 4 * unit], F32, name="room_c", align_bytes=64)
+        d_v0 = keep.tile([P, I], F32, name="d_v0")
+        d_v2 = keep.tile([P, I], F32, name="d_v2")
+        d_v3 = keep.tile([P, I], F32, name="d_v3", tag="d_v3")
+        b2 = keep.tile([P, I], F32, name="b2")
+        b3 = keep.tile([P, I], F32, name="b3", align_bytes=64)
 
         def wide(room, first):
             return room[:, first * unit : (first + 2) * unit]
@@ -166,56 +196,73 @@ def tile_attend_difference_apartvalues_lean_pl_kernel(
         def rounded(room, first, count=1):
             return room[:, first * unit : (first + count) * unit].bitcast(BF16)
 
-        pick(vb[0], list3, wide(room_x, 4))
-        score(0, (0, 1, 2))
-        pick(scores[0], list2, wide(room_x, 1))
-        score(1, (0, 2))
-        difference(va[0], wide(room_x, 4), wide(room_y, 3))
-        t_v0 = turn_values(wide(room_y, 3))
-        pick(scores[1], list2, wide(room_y, 1))
-        difference(scores[0], wide(room_x, 1), wide(room_x, 3))
-        scale_round(t_v0, vfac_sb, rounded(room_x, 2))
-        t_w0 = turn_weights(wide(room_x, 3))
-        pick(vb[1], list3, wide(room_y, 3))
-        difference(scores[1], wide(room_y, 1), wide(room_x, 0))
-        scale_round(t_w0, wfac_sb, rounded(room_y, 2))
-        t_w1 = turn_weights(wide(room_x, 0))
-        pick(vb[2], list3, wide(room_x, 3))
-        difference(va[1], wide(room_y, 3), wide(room_y, 0))
-        scale_round(t_w1, wfac_sb, rounded(room_y, 3))
-        t_v1 = turn_values(wide(room_y, 0))
-        w_mx = quantise(rounded(room_y, 2, 2), "w")
-        pick(vb[3], list3, wide(room_y, 0))
-        difference(va[2], wide(room_x, 3), wide(room_y, 4))
-        scale_round(t_v1, vfac_sb, rounded(room_x, 3))
-        t_v2 = turn_values(wide(room_y, 4))
-        v01_mx = quantise(rounded(room_x, 2, 2), "v01")
-        product(0, v01_mx, 0, w_mx)
-        product(1, v01_mx, P, w_mx)
-        difference(va[3], wide(room_y, 0), wide(room_x, 4))
-        scale_round(t_v2, vfac_sb, rounded(room_y, 0))
-        t_v3 = turn_values(wide(room_x, 4))
-        product(2, quantise(rounded(room_y, 0), "v2"), 0, w_mx)
-        nc.sync.dma_start(out=out_j[:, : PACK - 1, :], in_=o_sb[:, : PACK - 1, :])
-        scale_round(t_v3, vfac_sb, rounded(room_y, 1))
-        product(3, quantise(rounded(room_y, 1), "v3"), 0, w_mx)
-        nc.sync.dma_start(out=out_j[:, PACK - 1, :], in_=o_sb[:, PACK - 1, :])
+        on_vector, on_scalar = nc.vector.tensor_copy, nc.scalar.copy
+        pick(vb[0], list3, wide(room_a, 0))
+        scores.append(keep.tile([P, T], F32, name="scores1", tag="vb0", align_bytes=64))
+        score(0, 0, on_vector)
+        score(0, 1, on_vector)
+        score(1, 0, on_vector)
+        score(1, 1, on_scalar)
+        score(0, 2, on_vector)
+        score(0, 3, on_scalar)
+        pick(scores[0], list2, wide(room_b, 0))
+        score(1, 2, on_vector)
+        score(1, 3, on_scalar)
+        difference(va[0], wide(room_a, 0), d_v0[:])
+        difference(scores[0], wide(room_b, 0), wide(room_a, 1))
+        t_w0 = turn_weights(wide(room_a, 1))
+        pick(vb[1], list3, wide(room_c, 1))
+        t_v0 = turn_values(d_v0[:], "vb1")
+        pick(scores[1], list2, d_v0[:], sign=-1.0)
+        t_w1 = ps_a.tile([P, PACK, P], F32, name="t_w1", tag="acc")
+        turn_and_add(t_w1, d_v0[:], True)
+        difference(va[1], wide(room_c, 1), wide(room_b, 1))
+        scale_round(t_w0, wfac_sb, rounded(room_c, 2))
+        scale_round(t_v0, vfac_sb, rounded(room_c, 1))
+        t_v1 = turn_values(wide(room_b, 1), "size1")
+        pick(vb[2], list3, b2[:])
+        plus = keep.tile([P, I], F32, name="plus", tag="vb2", align_bytes=64)
+        pick(scores[1], list1, plus[:])
+        turn_and_add(t_w1, plus[:], False)
+        scale_round(t_v1, vfac_sb, rounded(room_c, 0))
+        difference(va[2], b2[:], d_v2[:])
+        v10_mx = quantise(rounded(room_c, 0, 2), "v10")
+        pick(vb[3], list3, b3[:])
+        t_v2 = turn_values(d_v2[:], "vb3")
+        scale_round(t_w1, wfac_sb, rounded(room_c, 3))
+        w_mx = quantise(rounded(room_c, 2, 2), "w")
+        product(0, v10_mx, P, w_mx)
+        product(1, v10_mx, 0, w_mx)
+        difference(va[3], b3[:], d_v3[:], parts=2)
+        t_v3 = turn_values(d_v3[:], "size3", parts=2)
+        o_sb = keep.tile([P, PACK, Q], F32, name="o_sb", tag="d_v3")
+        hand_out(slice(0, 2), (0, 1))
+        scale_round(t_v2, vfac_sb, rounded(b3, 1))
+        product(2, quantise(rounded(b3, 1), "v2"), 0, w_mx)
+        scale_round(t_v3, vfac_sb, rounded(b3, 0))
+        product(3, quantise(rounded(b3, 0), "v3"), 0, w_mx)
 
-        o_bf = keep.tile([P, Q, PACK], BF16, name="o_bf", align_bytes=64)
-        nc.vector.tensor_copy(
-            out=o_bf[:].rearrange("p (c i) t -> p c t i", i=4),
-            in_=o_sb[:].rearrange("p t (c i) -> p c t i", i=4),
-        )
         o_codes = keep.tile([P, Q], U32, name="o_codes", align_bytes=64)
         o_scales = keep.tile([P, Q], U8, name="o_scales", align_bytes=64)
-        nc.vector.quantize_mx(
-            out=o_codes[:].bitcast(FP8X4), scales=o_scales[:], in_=o_bf[:].rearrange("p q t -> p (q t)")
+        o_bf = [keep.tile([P, P * PACK], BF16, name="o_bf%d" % h, align_bytes=64) for h in range(Q // P)]
+        nc.vector.tensor_copy(
+            out=o_bf[0][:].rearrange("p (c t) -> p c t", t=PACK), in_=res[0][:].rearrange("p t c -> p c t")
         )
+        nc.scalar.copy(
+            out=o_bf[1][:].rearrange("p (c t) -> p c t", t=PACK), in_=res[1][:].rearrange("p t c -> p c t")
+        )
+        for h in range(Q // P):
+            nc.vector.quantize_mx(
+                out=o_codes[:, h * P : (h + 1) * P].bitcast(FP8X4),
+                scales=o_scales[:, h * P : (h + 1) * P],
+                in_=o_bf[h][:],
+            )
+        hand_out(slice(2, PACK), (1, 0))
         nc.sync.dma_start(
             out=out_1[0].rearrange("p q t -> p (q t)").bitcast(I32), in_=o_codes[:].bitcast(I32)
         )
         for g in range(4):
-            queue = nc.scalar if g % 2 == 0 else nc.sync
+            queue = nc.scalar if g >= 2 else nc.sync
             queue.dma_start(
                 out=out_2[0, 4 * g : 4 * g + 4, :].bitcast(I32),
                 in_=o_scales[32 * g : 32 * g + 4, :].bitcast(I32),

@@ -58,8 +58,8 @@ def tile_attend_difference_apartvalues_lean_pl_kernel(
         nc.sync.dma_start(list2[:], offs2)
         nc.sync.dma_start(list1[:], offs)
         nc.sync.dma_start(out=va[0][:], in_=vals_j[:, 0, :])
-        nc.gpsimd.dma_start(out=wfac_sb[:], in_=wfac.rearrange("o (p t) -> (o p) t", t=PACK))
-        nc.gpsimd.dma_start(out=vfac_sb[:], in_=vfac.rearrange("o (p t) -> (o p) t", t=PACK))
+        nc.sync.dma_start(out=wfac_sb[:], in_=wfac.rearrange("o (p t) -> (o p) t", t=PACK))
+        nc.sync.dma_start(out=vfac_sb[:], in_=vfac.rearrange("o (p t) -> (o p) t", t=PACK))
         for j in range(1, PACK):
             nc.sync.dma_start(out=vb[j][:], in_=vals2_j[:, j, :])
             nc.sync.dma_start(out=va[j][:], in_=vals_j[:, j, :])
@@ -152,28 +152,27 @@ def tile_attend_difference_apartvalues_lean_pl_kernel(
                 op=ALU.mult,
             )
 
-        def quantise(src, name):
+        def quantise(src, name, tag):
             width = src.shape[1] // PACK
-            codes = keep.tile([P, width], U32, name=name + "_codes", align_bytes=64)
+            codes = keep.tile([P, width], U32, name=name + "_codes", tag=tag, align_bytes=64)
             scales = keep.tile([P, width], U8, name=name + "_scales", align_bytes=64)
             nc.vector.quantize_mx(out=codes[:].bitcast(FP8X4), scales=scales[:], in_=src)
-            return codes, scales
+            return [(codes[:, c : c + P], scales[:, c : c + P]) for c in range(0, width, P)]
 
         out_j = out_0.rearrange("(p j) q -> p j q", j=PACK)
 
         res = [ps_o.tile([P, PACK, P], F32, name="res%d" % h) for h in range(Q // P)]
 
-        def product(j, v_mx, first, w_mx):
-            for h in range(Q // P):
-                nc.tensor.matmul_mx(
-                    out=res[h][:, j, :],
-                    lhsT=v_mx[0][:, first : first + P].bitcast(FP8X4),
-                    lhsT_scale=v_mx[1][:, first : first + P],
-                    rhs=w_mx[0][:, h * P : (h + 1) * P].bitcast(FP8X4),
-                    rhs_scale=w_mx[1][:, h * P : (h + 1) * P],
-                    start=True,
-                    stop=True,
-                )
+        def product(j, h, v_mx, w_mx):
+            nc.tensor.matmul_mx(
+                out=res[h][:, j, :],
+                lhsT=v_mx[0].bitcast(FP8X4),
+                lhsT_scale=v_mx[1],
+                rhs=w_mx[0].bitcast(FP8X4),
+                rhs_scale=w_mx[1],
+                start=True,
+                stop=True,
+            )
 
         def hand_out(tiles, banks):
             for h in banks:
@@ -187,7 +186,6 @@ def tile_attend_difference_apartvalues_lean_pl_kernel(
         d_v0 = keep.tile([P, I], F32, name="d_v0")
         d_v2 = keep.tile([P, I], F32, name="d_v2")
         d_v3 = keep.tile([P, I], F32, name="d_v3", tag="d_v3")
-        b2 = keep.tile([P, I], F32, name="b2")
         b3 = keep.tile([P, I], F32, name="b3", align_bytes=64)
 
         def wide(room, first):
@@ -207,40 +205,44 @@ def tile_attend_difference_apartvalues_lean_pl_kernel(
         score(0, 3, on_scalar)
         pick(scores[0], list2, wide(room_b, 0))
         score(1, 2, on_vector)
-        score(1, 3, on_scalar)
+        score(1, 3, on_vector)
         difference(va[0], wide(room_a, 0), d_v0[:])
         difference(scores[0], wide(room_b, 0), wide(room_a, 1))
         t_w0 = turn_weights(wide(room_a, 1))
-        pick(vb[1], list3, wide(room_c, 1))
+        pick(vb[1], list3, wide(room_c, 0))
         t_v0 = turn_values(d_v0[:], "vb1")
         pick(scores[1], list2, d_v0[:], sign=-1.0)
         t_w1 = ps_a.tile([P, PACK, P], F32, name="t_w1", tag="acc")
         turn_and_add(t_w1, d_v0[:], True)
-        difference(va[1], wide(room_c, 1), wide(room_b, 1))
-        scale_round(t_w0, wfac_sb, rounded(room_c, 2))
-        scale_round(t_v0, vfac_sb, rounded(room_c, 1))
-        t_v1 = turn_values(wide(room_b, 1), "size1")
-        pick(vb[2], list3, b2[:])
-        plus = keep.tile([P, I], F32, name="plus", tag="vb2", align_bytes=64)
-        pick(scores[1], list1, plus[:])
-        turn_and_add(t_w1, plus[:], False)
-        scale_round(t_v1, vfac_sb, rounded(room_c, 0))
-        difference(va[2], b2[:], d_v2[:])
-        v10_mx = quantise(rounded(room_c, 0, 2), "v10")
+        difference(va[1], wide(room_c, 0), wide(room_b, 1))
+        scale_round(t_w0, wfac_sb, rounded(room_c, 1))
+        scale_round(t_v0, vfac_sb, rounded(room_c, 0))
+        pick(vb[2], list3, wide(room_c, 2))
+        t_v1 = turn_values(wide(room_b, 1), "vb2")
+        pick(scores[1], list1, wide(room_b, 1))
+        turn_and_add(t_w1, wide(room_b, 1), False)
+        difference(va[2], wide(room_c, 2), d_v2[:])
+        scale_round(t_v1, vfac_sb, rounded(room_c, 3))
+        v0_mx, w0_mx = quantise(rounded(room_c, 0, 2), "v0w0", "va2")
+        (v1_mx,) = quantise(rounded(room_c, 3), "v1", "v1")
+        product(0, 0, v0_mx, w0_mx)
+        product(1, 0, v1_mx, w0_mx)
         pick(vb[3], list3, b3[:])
         t_v2 = turn_values(d_v2[:], "vb3")
-        scale_round(t_w1, wfac_sb, rounded(room_c, 3))
-        w_mx = quantise(rounded(room_c, 2, 2), "w")
-        product(0, v10_mx, P, w_mx)
-        product(1, v10_mx, 0, w_mx)
+        scale_round(t_w1, wfac_sb, rounded(room_c, 2))
         difference(va[3], b3[:], d_v3[:], parts=2)
         t_v3 = turn_values(d_v3[:], "size3", parts=2)
+        scale_round(t_v2, vfac_sb, rounded(b3, 0))
+        (w1_mx,) = quantise(rounded(room_c, 2), "w1", "va3")
+        product(0, 1, v0_mx, w1_mx)
+        product(1, 1, v1_mx, w1_mx)
         o_sb = keep.tile([P, PACK, Q], F32, name="o_sb", tag="d_v3")
         hand_out(slice(0, 2), (0, 1))
-        scale_round(t_v2, vfac_sb, rounded(b3, 1))
-        product(2, quantise(rounded(b3, 1), "v2"), 0, w_mx)
-        scale_round(t_v3, vfac_sb, rounded(b3, 0))
-        product(3, quantise(rounded(b3, 0), "v3"), 0, w_mx)
+        scale_round(t_v3, vfac_sb, rounded(b3, 1))
+        v2_mx, v3_mx = quantise(rounded(b3, 0, 2), "v2v3", "v2v3")
+        for h, w_mx in enumerate((w0_mx, w1_mx)):
+            product(2, h, v2_mx, w_mx)
+            product(3, h, v3_mx, w_mx)
 
         o_codes = keep.tile([P, Q], U32, name="o_codes", align_bytes=64)
         o_scales = keep.tile([P, Q], U8, name="o_scales", align_bytes=64)

@@ -28,6 +28,7 @@ def tile_attend_difference_apartvalues_lean_pl_kernel(
     nc = tc.nc
     with ExitStack() as ctx:
         keep = ctx.enter_context(tc.tile_pool(name="keep", bufs=1))
+        last = ctx.enter_context(tc.tile_pool(name="last", bufs=1))
         ps_a = ctx.enter_context(tc.psum_pool(name="ps_a", bufs=3))
         ps_t = ctx.enter_context(tc.psum_pool(name="ps_t", bufs=3))
         ps_o = ctx.enter_context(tc.psum_pool(name="ps_o", bufs=1))
@@ -40,7 +41,8 @@ def tile_attend_difference_apartvalues_lean_pl_kernel(
         k_scales = keep.tile([P, T], U8, name="k_scales", align_bytes=64)
         wfac_sb = keep.tile([P, PACK], F32, name="wfac_sb")
         vfac_sb = keep.tile([P, PACK], F32, name="vfac_sb")
-        va = [keep.tile([P, T], F32, name="va%d" % j, tag="va%d" % j, align_bytes=64) for j in range(PACK)]
+        va = [keep.tile([P, T], F32, name="va%d" % j, tag="va%d" % j, align_bytes=64) for j in range(PACK - 1)]
+        va.append(last.tile([P, T], F32, name="va3", offset=0, align_bytes=64))
         vb = [keep.tile([P, X], F32, name="vb%d" % j, tag="vb%d" % j, align_bytes=64) for j in range(PACK)]
         vals_j = vals.rearrange("(p j) t -> p j t", j=PACK)
         vals2_j = vals2.rearrange("(p j) t -> p j t", j=PACK)
@@ -152,9 +154,8 @@ def tile_attend_difference_apartvalues_lean_pl_kernel(
                 op=ALU.mult,
             )
 
-        def quantise(src, name, tag):
+        def quantise(src, name, codes):
             width = src.shape[1] // PACK
-            codes = keep.tile([P, width], U32, name=name + "_codes", tag=tag, align_bytes=64)
             scales = keep.tile([P, width], U8, name=name + "_scales", align_bytes=64)
             nc.vector.quantize_mx(out=codes[:].bitcast(FP8X4), scales=scales[:], in_=src)
             return [(codes[:, c : c + P], scales[:, c : c + P]) for c in range(0, width, P)]
@@ -185,7 +186,7 @@ def tile_attend_difference_apartvalues_lean_pl_kernel(
         room_c = keep.tile([P, 4 * unit], F32, name="room_c", align_bytes=64)
         d_v0 = keep.tile([P, I], F32, name="d_v0")
         d_v2 = keep.tile([P, I], F32, name="d_v2")
-        d_v3 = keep.tile([P, I], F32, name="d_v3", tag="d_v3")
+        a3 = keep.tile([P, I], F32, name="a3")
         b3 = keep.tile([P, I], F32, name="b3", align_bytes=64)
 
         def wide(room, first):
@@ -223,26 +224,41 @@ def tile_attend_difference_apartvalues_lean_pl_kernel(
         turn_and_add(t_w1, wide(room_b, 1), False)
         difference(va[2], wide(room_c, 2), d_v2[:])
         scale_round(t_v1, vfac_sb, rounded(room_c, 3))
-        v0_mx, w0_mx = quantise(rounded(room_c, 0, 2), "v0w0", "va2")
-        (v1_mx,) = quantise(rounded(room_c, 3), "v1", "v1")
+        v0_mx, w0_mx = quantise(rounded(room_c, 0, 2), "v0w0", keep.tile([P, 2 * P], U32, name="v0w0_codes", tag="va2", align_bytes=64))
+        (v1_mx,) = quantise(rounded(room_c, 3), "v1", keep.tile([P, P], U32, name="v1_codes", align_bytes=64))
         product(0, 0, v0_mx, w0_mx)
         product(1, 0, v1_mx, w0_mx)
-        pick(vb[3], list3, b3[:])
+        pick(vb[3], list3, b3[:], sign=-1.0)
+        t_v3 = ps_a.tile([P, PACK, P], F32, name="t_v3", tag="acc")
+        turn_and_add(t_v3, b3[:], True)
         t_v2 = turn_values(d_v2[:], "vb3")
         scale_round(t_w1, wfac_sb, rounded(room_c, 2))
-        difference(va[3], b3[:], d_v3[:], parts=2)
-        t_v3 = turn_values(d_v3[:], "size3", parts=2)
-        scale_round(t_v2, vfac_sb, rounded(b3, 0))
-        (w1_mx,) = quantise(rounded(room_c, 2), "w1", "va3")
+        nc.vector.tensor_copy(out=a3[:, : I // 2], in_=va[3][:].indirect(list1[:, : I // 32]))
+        nc.scalar.activation(out=a3[:, I // 2 :], in_=va[3][:].indirect(list1[:, I // 32 :]), func=ACT.Copy)
+        turn_and_add(t_v3, a3[:], False)
+        w1_codes = last.tile([P, P], U32, name="w1_codes", offset=0, align_bytes=64)
+        (w1_mx,) = quantise(rounded(room_c, 2), "w1", w1_codes)
         product(0, 1, v0_mx, w1_mx)
         product(1, 1, v1_mx, w1_mx)
-        o_sb = keep.tile([P, PACK, Q], F32, name="o_sb", tag="d_v3")
-        hand_out(slice(0, 2), (0, 1))
-        scale_round(t_v3, vfac_sb, rounded(b3, 1))
-        v2_mx, v3_mx = quantise(rounded(b3, 0, 2), "v2v3", "v2v3")
-        for h, w_mx in enumerate((w0_mx, w1_mx)):
-            product(2, h, v2_mx, w_mx)
-            product(3, h, v3_mx, w_mx)
+        size3 = keep.tile([P, P, PACK], F32, name="size3")
+        nc.scalar.activation(out=size3[:], in_=t_v3[:].rearrange("p t c -> p c t"), func=ACT.Abs)
+        v2_bf = last.tile([P, I], BF16, name="v2_bf", offset=1024, align_bytes=64)
+        scale_round(t_v2, vfac_sb, v2_bf[:])
+        (v2_mx,) = quantise(v2_bf[:], "v2", keep.tile([P, P], U32, name="v2_codes", align_bytes=64))
+        product(2, 0, v2_mx, w0_mx)
+        product(2, 1, v2_mx, w1_mx)
+        o_sb = keep.tile([P, PACK, Q], F32, name="o_sb")
+        hand_out(slice(0, PACK - 1), (0, 1))
+        v3_bf = keep.tile([P, I], BF16, name="v3_bf", align_bytes=64)
+        nc.vector.tensor_tensor(
+            out=v3_bf[:].rearrange("p (c t) -> p c t", t=PACK),
+            in0=size3[:],
+            in1=vfac_sb[:].unsqueeze(1).to_broadcast([P, P, PACK]),
+            op=ALU.mult,
+        )
+        (v3_mx,) = quantise(v3_bf[:], "v3", keep.tile([P, P], U32, name="v3_codes", align_bytes=64))
+        product(3, 0, v3_mx, w0_mx)
+        product(3, 1, v3_mx, w1_mx)
 
         o_codes = keep.tile([P, Q], U32, name="o_codes", align_bytes=64)
         o_scales = keep.tile([P, Q], U8, name="o_scales", align_bytes=64)
@@ -259,7 +275,7 @@ def tile_attend_difference_apartvalues_lean_pl_kernel(
                 scales=o_scales[:, h * P : (h + 1) * P],
                 in_=o_bf[h][:],
             )
-        hand_out(slice(2, PACK), (1, 0))
+        hand_out(slice(PACK - 1, PACK), (1, 0))
         nc.sync.dma_start(
             out=out_1[0].rearrange("p q t -> p (q t)").bitcast(I32), in_=o_codes[:].bitcast(I32)
         )

from contextlib import ExitStack

import concourse.mybir as mybir
from concourse.masks import make_identity

D, T, I, Q, E, X = 512, 2048, 512, 256, 512, 1024
FLOPS = 2 * D * Q * T + 2 * I * E * Q

F32 = mybir.dt.float32
BF16 = mybir.dt.bfloat16
I32 = mybir.dt.int32
U32 = mybir.dt.uint32
U16 = mybir.dt.uint16
U8 = mybir.dt.uint8
FP8X4 = mybir.dt.float8_e4m3fn_x4
FP4X4 = mybir.dt.float4_e2m1fn_x4
ALU = mybir.AluOpType
ACT = mybir.ActivationFunctionType

P = 128
PACK = 4
BANK = 512


def tile_attend_difference_apartvalues_lean_pl_kernel(
    tc, query, keys_words, keys_scales, wfac, vals, vals2, vfac, offs, offs2, offs3, out_0, out_1, out_2
):
    nc = tc.nc
    with ExitStack() as ctx:
        keep = ctx.enter_context(tc.tile_pool(name="keep", bufs=1))
        last = ctx.enter_context(tc.tile_pool(name="last", bufs=1))
        ps_a = ctx.enter_context(tc.psum_pool(name="ps_a", bufs=3))
        ps_t = ctx.enter_context(tc.psum_pool(name="ps_t", bufs=3))
        ps_o = ctx.enter_context(tc.psum_pool(name="ps_o", bufs=1))

        list1 = keep.tile([P, I // 16], U16, name="list1")
        list2 = keep.tile([P, I // 16], U16, name="list2")
        list3 = keep.tile([P, I // 16], U16, name="list3")
        q_raw = keep.tile([P, PACK, Q], F32, name="q_raw")
        k_words = keep.tile([P, 2 * T], U8, name="k_words", align_bytes=64)
        k_scales = keep.tile([P, T], U8, name="k_scales", align_bytes=64)
        wfac_sb = keep.tile([P, PACK], F32, name="wfac_sb")
        vfac_sb = keep.tile([P, PACK], F32, name="vfac_sb")
        va = [keep.tile([P, T], F32, name="va%d" % j, tag="va%d" % j, align_bytes=64) for j in range(PACK - 1)]
        va.append(last.tile([P, T], F32, name="va3", offset=0, align_bytes=64))
        vb = [keep.tile([P, X], F32, name="vb%d" % j, tag="vb%d" % j, align_bytes=64) for j in range(PACK)]
        vals_j = vals.rearrange("(p j) t -> p j t", j=PACK)
        vals2_j = vals2.rearrange("(p j) t -> p j t", j=PACK)

        nc.sync.dma_start(out=q_raw[:], in_=query.rearrange("(p j) q -> p j q", j=PACK))
        for g in range(4):
            nc.sync.dma_start(
                out=k_scales[32 * g : 32 * g + 4, :].bitcast(I32),
                in_=keys_scales[0, 4 * g : 4 * g + 4, :].bitcast(I32),
            )
        nc.sync.dma_start(out=k_words[:, :T].bitcast(I32), in_=keys_words[0, :, :T].bitcast(I32))
        nc.sync.dma_start(list3[:], offs3)
        nc.sync.dma_start(out=vb[0][:], in_=vals2_j[:, 0, :])
        nc.sync.dma_start(out=k_words[:, T:].bitcast(I32), in_=keys_words[0, :, T:].bitcast(I32))
        nc.sync.dma_start(list2[:], offs2)
        nc.sync.dma_start(list1[:], offs)
        nc.sync.dma_start(out=va[0][:], in_=vals_j[:, 0, :])
        nc.sync.dma_start(out=wfac_sb[:], in_=wfac.rearrange("o (p t) -> (o p) t", t=PACK))
        nc.sync.dma_start(out=vfac_sb[:], in_=vfac.rearrange("o (p t) -> (o p) t", t=PACK))
        for j in range(1, PACK):
            nc.sync.dma_start(out=vb[j][:], in_=vals2_j[:, j, :])
            nc.sync.dma_start(out=va[j][:], in_=vals_j[:, j, :])

        ident = keep.tile([P, P], F32, name="ident")
        make_identity(nc, ident[:])

        q_bf = keep.tile([P, Q * PACK], BF16, name="q_bf", align_bytes=64)
        q_codes = keep.tile([P, Q], U32, name="q_codes", align_bytes=64)
        q_scales = keep.tile([P, Q], U8, name="q_scales", align_bytes=64)
        for h, rounding in enumerate((nc.vector.tensor_copy, nc.scalar.copy)):
            rounding(
                out=q_bf[:, h * BANK : (h + 1) * BANK].rearrange("p (c i t) -> p c t i", i=4, t=PACK),
                in_=q_raw[:, :, h * P : (h + 1) * P].rearrange("p t (c i) -> p c t i", i=4),
            )
        for h in range(Q // P):
            nc.vector.quantize_mx(
                out=q_codes[:, h * P : (h + 1) * P].bitcast(FP8X4),
                scales=q_scales[:, h * P : (h + 1) * P],
                in_=q_bf[:, h * BANK : (h + 1) * BANK],
            )

        scores = [keep.tile([P, T], F32, name="scores0")]

        def score(h, c, emptying):
            rows = slice(h * P, (h + 1) * P)
            acc = ps_a.tile([P, BANK], F32, name="acc", tag="acc")
            nc.tensor.matmul_mx(
                out=acc[:],
                lhsT=q_codes[:, rows].bitcast(FP8X4),
                lhsT_scale=q_scales[:, rows],
                rhs=k_words[:, 2 * BANK * c : 2 * BANK * (c + 1)].bitcast(FP4X4),
                rhs_scale=k_scales[:, BANK * c : BANK * (c + 1)],
                start=True,
                stop=True,
            )
            emptying(out=scores[h][:, BANK * c : BANK * (c + 1)], in_=acc[:])

        def pick(window, offsets, got, sign=1.0):
            nc.scalar.activation(out=got, in_=window[:].indirect(offsets[:]), func=ACT.Copy, scale=sign)

        def difference(window, other, diff, parts=1):
            width = I // parts
            for n in range(parts):
                cols = slice(n * width, (n + 1) * width)
                nc.vector.tensor_tensor(
                    out=diff[:, cols],
                    in0=window[:].indirect(list1[:, n * width // 16 : (n + 1) * width // 16]),
                    in1=other[:, cols],
                    op=ALU.subtract,
                )

        def turn_and_add(bank, term, first):
            for t in range(PACK):
                nc.tensor.matmul(
                    bank[:, t, :],
                    term[:, t::PACK],
                    ident[:],
                    start=first and t == 0,
                    stop=not first and t == PACK - 1,
                    is_transpose=True,
                )

        def turn(places):
            turned = ps_t.tile([P, PACK, P], F32, name="turned")
            for t in range(PACK):
                nc.tensor.transpose(turned[:, t, :], places[t], ident[:])
            return turned

        def turn_weights(diff):
            return turn([diff[:, t::PACK] for t in range(PACK)])

        def turn_values(diff, tag, parts=1):
            size = keep.tile([P, PACK, P], F32, name="size", tag=tag, align_bytes=64)
            width = P // parts
            for n in range(parts):
                rows = slice(n * width, (n + 1) * width)
                nc.scalar.activation(
                    out=size[:].rearrange("p t s -> p s t")[:, rows, :],
                    in_=diff.rearrange("p (s t) -> p s t", t=PACK)[:, rows, :],
                    func=ACT.Abs,
                )
            return turn([size[:, t, :] for t in range(PACK)])

        def scale_round(turned, factor, dst):
            nc.vector.tensor_tensor(
                out=dst.rearrange("p (c t) -> p c t", t=PACK),
                in0=turned[:].rearrange("p t c -> p c t"),
                in1=factor[:].unsqueeze(1).to_broadcast([P, P, PACK]),
                op=ALU.mult,
            )

        def quantise(src, name, codes):
            width = src.shape[1] // PACK
            scales = keep.tile([P, width], U8, name=name + "_scales", align_bytes=64)
            nc.vector.quantize_mx(out=codes[:].bitcast(FP8X4), scales=scales[:], in_=src)
            return [(codes[:, c : c + P], scales[:, c : c + P]) for c in range(0, width, P)]

        out_j = out_0.rearrange("(p j) q -> p j q", j=PACK)

        res = [ps_o.tile([P, PACK, P], F32, name="res%d" % h) for h in range(Q // P)]

        def product(j, h, v_mx, w_mx):
            nc.tensor.matmul_mx(
                out=res[h][:, j, :],
                lhsT=v_mx[0].bitcast(FP8X4),
                lhsT_scale=v_mx[1],
                rhs=w_mx[0].bitcast(FP8X4),
                rhs_scale=w_mx[1],
                start=True,
                stop=True,
            )

        def hand_out(tiles, banks):
            for h in banks:
                nc.scalar.copy(out=o_sb[:, tiles, h * P : (h + 1) * P], in_=res[h][:, tiles, :])
            nc.sync.dma_start(out=out_j[:, tiles, :], in_=o_sb[:, tiles, :])

        unit = I // 2
        room_a = keep.tile([P, 3 * unit], F32, name="room_a")
        room_b = keep.tile([P, 3 * unit], F32, name="room_b")
        room_c = keep.tile([P, 4 * unit], F32, name="room_c", align_bytes=64)
        d_v0 = keep.tile([P, I], F32, name="d_v0")
        d_v2 = keep.tile([P, I], F32, name="d_v2")
        a3 = keep.tile([P, I], F32, name="a3")
        b3 = keep.tile([P, I], F32, name="b3", align_bytes=64)

        def wide(room, first):
            return room[:, first * unit : (first + 2) * unit]

        def rounded(room, first, count=1):
            return room[:, first * unit : (first + count) * unit].bitcast(BF16)

        on_vector, on_scalar = nc.vector.tensor_copy, nc.scalar.copy
        pick(vb[0], list3, wide(room_a, 0))
        scores.append(keep.tile([P, T], F32, name="scores1", tag="vb0", align_bytes=64))
        score(0, 0, on_vector)
        score(0, 1, on_vector)
        score(1, 0, on_vector)
        score(1, 1, on_scalar)
        score(0, 2, on_vector)
        score(0, 3, on_scalar)
        pick(scores[0], list2, wide(room_b, 0))
        score(1, 2, on_vector)
        score(1, 3, on_vector)
        difference(va[0], wide(room_a, 0), d_v0[:])
        difference(scores[0], wide(room_b, 0), wide(room_a, 1))
        t_w0 = turn_weights(wide(room_a, 1))
        pick(vb[1], list3, wide(room_c, 0))
        t_v0 = turn_values(d_v0[:], "vb1")
        pick(scores[1], list2, d_v0[:], sign=-1.0)
        t_w1 = ps_a.tile([P, PACK, P], F32, name="t_w1", tag="acc")
        turn_and_add(t_w1, d_v0[:], True)
        difference(va[1], wide(room_c, 0), wide(room_b, 1))
        scale_round(t_w0, wfac_sb, rounded(room_c, 1))
        scale_round(t_v0, vfac_sb, rounded(room_c, 0))
        pick(vb[2], list3, wide(room_c, 2))
        t_v1 = turn_values(wide(room_b, 1), "vb2")
        pick(scores[1], list1, wide(room_b, 1))
        turn_and_add(t_w1, wide(room_b, 1), False)
        difference(va[2], wide(room_c, 2), d_v2[:])
        scale_round(t_v1, vfac_sb, rounded(room_c, 3))
        v0_mx, w0_mx = quantise(rounded(room_c, 0, 2), "v0w0", keep.tile([P, 2 * P], U32, name="v0w0_codes", tag="va2", align_bytes=64))
        (v1_mx,) = quantise(rounded(room_c, 3), "v1", keep.tile([P, P], U32, name="v1_codes", align_bytes=64))
        product(0, 0, v0_mx, w0_mx)
        product(1, 0, v1_mx, w0_mx)
        pick(vb[3], list3, b3[:], sign=-1.0)
        t_v3 = ps_a.tile([P, PACK, P], F32, name="t_v3", tag="acc")
        turn_and_add(t_v3, b3[:], True)
        t_v2 = turn_values(d_v2[:], "vb3")
        scale_round(t_w1, wfac_sb, rounded(room_c, 2))
        nc.vector.tensor_copy(out=a3[:, : I // 2], in_=va[3][:].indirect(list1[:, : I // 32]))
        nc.scalar.activation(out=a3[:, I // 2 :], in_=va[3][:].indirect(list1[:, I // 32 :]), func=ACT.Copy)
        turn_and_add(t_v3, a3[:], False)
        w1_codes = last.tile([P, P], U32, name="w1_codes", offset=0, align_bytes=64)
        (w1_mx,) = quantise(rounded(room_c, 2), "w1", w1_codes)
        product(0, 1, v0_mx, w1_mx)
        product(1, 1, v1_mx, w1_mx)
        size3 = keep.tile([P, P, PACK], F32, name="size3")
        nc.scalar.activation(out=size3[:], in_=t_v3[:].rearrange("p t c -> p c t"), func=ACT.Abs)
        v2_bf = last.tile([P, I], BF16, name="v2_bf", offset=1024, align_bytes=64)
        scale_round(t_v2, vfac_sb, v2_bf[:])
        (v2_mx,) = quantise(v2_bf[:], "v2", keep.tile([P, P], U32, name="v2_codes", align_bytes=64))
        product(2, 0, v2_mx, w0_mx)
        product(2, 1, v2_mx, w1_mx)
        o_sb = keep.tile([P, PACK, Q], F32, name="o_sb")
        hand_out(slice(0, PACK - 1), (0, 1))
        v3_bf = keep.tile([P, I], BF16, name="v3_bf", align_bytes=64)
        nc.vector.tensor_tensor(
            out=v3_bf[:].rearrange("p (c t) -> p c t", t=PACK),
            in0=size3[:],
            in1=vfac_sb[:].unsqueeze(1).to_broadcast([P, P, PACK]),
            op=ALU.mult,
        )
        (v3_mx,) = quantise(v3_bf[:], "v3", keep.tile([P, P], U32, name="v3_codes", align_bytes=64))
        product(3, 0, v3_mx, w0_mx)
        product(3, 1, v3_mx, w1_mx)

        o_codes = keep.tile([P, Q], U32, name="o_codes", align_bytes=64)
        o_scales = keep.tile([P, Q], U8, name="o_scales", align_bytes=64)
        o_bf = [keep.tile([P, P * PACK], BF16, name="o_bf%d" % h, align_bytes=64) for h in range(Q // P)]
        nc.vector.tensor_copy(
            out=o_bf[0][:].rearrange("p (c t) -> p c t", t=PACK), in_=res[0][:].rearrange("p t c -> p c t")
        )
        nc.scalar.copy(
            out=o_bf[1][:].rearrange("p (c t) -> p c t", t=PACK), in_=res[1][:].rearrange("p t c -> p c t")
        )
        for h in range(Q // P):
            nc.vector.quantize_mx(
                out=o_codes[:, h * P : (h + 1) * P].bitcast(FP8X4),
                scales=o_scales[:, h * P : (h + 1) * P],
                in_=o_bf[h][:],
            )
        hand_out(slice(PACK - 1, PACK), (1, 0))
        nc.sync.dma_start(
            out=out_1[0].rearrange("p q t -> p (q t)").bitcast(I32), in_=o_codes[:].bitcast(I32)
        )
        for g in range(4):
            queue = nc.scalar if g >= 2 else nc.sync
            queue.dma_start(
                out=out_2[0, 4 * g : 4 * g + 4, :].bitcast(I32),
                in_=o_scales[32 * g : 32 * g + 4, :].bitcast(I32),
            )
